import numpy as np
import ml_dtypes

BF16 = ml_dtypes.bfloat16


def bf(x):
    return np.asarray(x, np.float32).astype(BF16)


def f32(x):
    return np.asarray(x, np.float32)


def f64(x):
    return np.asarray(x).astype(np.float64)


def striped(idx):
    return np.tile(idx.reshape(-1, 16).T, (8, 1))


def rows(idx, k):
    return np.tile(idx, (k, 1))


def look(tab, idx):
    return np.take_along_axis(f64(tab), rows(idx, len(tab)), axis=1)


K, S, D, V, N = 512, 256, 3, 64, 192


def setup_inputs():
    return {"tab": f32(np.random.standard_normal((K, S))), "x0": f32(np.random.standard_normal((K, V))), "offs": striped(np.random.permutation(S)[:N])}


def reference(tab, x0, offs):
    idx = offs[:16].T.reshape(-1)
    x = f64(x0)
    for d in range(D):
        x = np.minimum(x, look(tab, idx[d * V:(d + 1) * V]))
    return x

@@ -1,0 +1,42 @@
+import concourse.mybir as mybir
+
+F32 = mybir.dt.float32
+U16 = mybir.dt.uint16
+MIN = mybir.AluOpType.min
+
+P = 128
+LANES = 16
+NEIGHBOURS = 3
+FLOPS = 512 * 64 * NEIGHBOURS
+
+
+def tile_lookup_pool_min_out_kernel(tc, tab, x0, offs, out):
+    nc = tc.nc
+    rows, columns = tab.shape
+    width = x0.shape[1]
+    blocks = rows // P
+    tab_blocks = tab.rearrange("(p b) s -> b p s", b=blocks)
+    x0_rows = x0.rearrange("(p b) v -> p (b v)", b=blocks)
+    out_rows = out.rearrange("(p b) v -> p (b v)", b=blocks)
+    piece = width // LANES
+
+    with tc.tile_pool(name="held", bufs=1) as held:
+        offsets = held.tile([P, offs.shape[1]], U16, name="offsets")
+        nc.sync.dma_start(offsets[:], offs)
+        centre = held.tile([P, blocks * width], F32, name="centre")
+        nc.scalar.dma_start(centre[:], x0_rows)
+        windows = []
+        for b in range(blocks):
+            window = held.tile([P, columns], F32, name="window%d" % b)
+            nc.sync.dma_start(window[:], tab_blocks[b])
+            windows.append(window)
+
+        smallest = [held.tile([P, blocks * width], F32, name="smallest%d" % d) for d in range(NEIGHBOURS)]
+        for b in range(blocks):
+            mine = slice(b * width, (b + 1) * width)
+            so_far = centre
+            for d in range(NEIGHBOURS):
+                picked = windows[b][:].indirect(offsets[:, d * piece : (d + 1) * piece])
+                nc.vector.tensor_tensor(smallest[d][:, mine], picked, so_far[:, mine], MIN)
+                so_far = smallest[d]
+        nc.sync.dma_start(out_rows, smallest[-1][:])

@@ -28,15 +28,17 @@ def tile_lookup_pool_min_out_kernel(tc, tab, x0, offs, out):
         windows = []
         for b in range(blocks):
             window = held.tile([P, columns], F32, name="window%d" % b)
-            nc.sync.dma_start(window[:], tab_blocks[b])
+            queue = nc.sync if b % 2 == 0 else nc.scalar
+            queue.dma_start(window[:], tab_blocks[b])
             windows.append(window)
 
         smallest = [held.tile([P, blocks * width], F32, name="smallest%d" % d) for d in range(NEIGHBOURS)]
-        for b in range(blocks):
-            mine = slice(b * width, (b + 1) * width)
+        for pair in range(0, blocks, 2):
             so_far = centre
             for d in range(NEIGHBOURS):
-                picked = windows[b][:].indirect(offsets[:, d * piece : (d + 1) * piece])
-                nc.vector.tensor_tensor(smallest[d][:, mine], picked, so_far[:, mine], MIN)
+                for b in (pair, pair + 1):
+                    mine = slice(b * width, (b + 1) * width)
+                    picked = windows[b][:].indirect(offsets[:, d * piece : (d + 1) * piece])
+                    nc.vector.tensor_tensor(smallest[d][:, mine], picked, so_far[:, mine], MIN)
                 so_far = smallest[d]
         nc.sync.dma_start(out_rows, smallest[-1][:])

import concourse.mybir as mybir

F32 = mybir.dt.float32
U16 = mybir.dt.uint16
MIN = mybir.AluOpType.min

P = 128
LANES = 16
NEIGHBOURS = 3
FLOPS = 512 * 64 * NEIGHBOURS


def tile_lookup_pool_min_out_kernel(tc, tab, x0, offs, out):
    nc = tc.nc
    rows, columns = tab.shape
    width = x0.shape[1]
    blocks = rows // P
    tab_blocks = tab.rearrange("(p b) s -> b p s", b=blocks)
    x0_rows = x0.rearrange("(p b) v -> p (b v)", b=blocks)
    out_rows = out.rearrange("(p b) v -> p (b v)", b=blocks)
    piece = width // LANES

    with tc.tile_pool(name="held", bufs=1) as held:
        offsets = held.tile([P, offs.shape[1]], U16, name="offsets")
        nc.sync.dma_start(offsets[:], offs)
        centre = held.tile([P, blocks * width], F32, name="centre")
        nc.scalar.dma_start(centre[:], x0_rows)
        windows = []
        for b in range(blocks):
            window = held.tile([P, columns], F32, name="window%d" % b)
            queue = nc.sync if b % 2 == 0 else nc.scalar
            queue.dma_start(window[:], tab_blocks[b])
            windows.append(window)

        smallest = [held.tile([P, blocks * width], F32, name="smallest%d" % d) for d in range(NEIGHBOURS)]
        for pair in range(0, blocks, 2):
            so_far = centre
            for d in range(NEIGHBOURS):
                for b in (pair, pair + 1):
                    mine = slice(b * width, (b + 1) * width)
                    picked = windows[b][:].indirect(offsets[:, d * piece : (d + 1) * piece])
                    nc.vector.tensor_tensor(smallest[d][:, mine], picked, so_far[:, mine], MIN)
                so_far = smallest[d]
        nc.sync.dma_start(out_rows, smallest[-1][:])
